import numpy as np
import ml_dtypes


def mxq(x, axis, fmt="e4m3"):
    dtype, down = {"e4m3": (ml_dtypes.float8_e4m3fn, 7), "e5m2": (ml_dtypes.float8_e5m2, 14)}[fmt]
    v = np.moveaxis(np.asarray(x, np.float32).astype(ml_dtypes.bfloat16).astype(np.float64), axis, -1)
    blocks = v.reshape(v.shape[:-1] + (-1, 32))
    amax = np.abs(blocks).max(-1, keepdims=True)
    byte = np.maximum(np.where(amax > 0, np.frexp(amax)[1] - 1 + 127, 0) - down, 1)
    scale = np.exp2(byte - 127.0)
    codes = (blocks / scale).astype(np.float32).astype(dtype).astype(np.float64)
    return np.moveaxis((codes * scale).reshape(v.shape), -1, axis)


WIDE = False


def mx_kscale(k):
    if not WIDE:
        return np.ones(k)
    levels = np.array([10, -10, 5, -5, 0])
    if k % 512:
        return np.exp2(np.random.permutation(np.resize(levels, k // 32))).repeat(32)
    a = np.empty((k // 512, 16))
    for p in range(k // 512):
        a[p, :8] = np.random.permutation(np.resize(levels, 8))
        for g in range(8):
            far = levels[np.abs(levels - a[p, g]) >= 10]
            a[p, g + 8] = far[np.random.randint(len(far))]
    return np.exp2(a.ravel()).repeat(32)


def f64(x):
    return np.asarray(x).astype(np.float64)


def striped(idx):
    return np.tile(idx.reshape(-1, 16).T, (8, 1)).astype(np.uint16)


def unstriped(offs):
    return offs[:16].T.reshape(-1).astype(np.int64)


def pack_weight(w):
    k, n = w.shape
    w = f64(np.asarray(w, np.float32).astype(ml_dtypes.bfloat16)).reshape(k // 32, 32, n)
    amax = np.abs(w).max(1)
    byte = np.clip(np.where(amax > 0, np.frexp(amax)[1] - 1 + 127 - 7, 1), 1, 254)
    scaled = (w * np.exp2(127.0 - byte)[:, None, :]).reshape(k, n).astype(np.float32)
    words = np.ascontiguousarray(scaled.reshape(k // 512, 128, 4, n).transpose(0, 1, 3, 2)).astype(ml_dtypes.float8_e4m3fn).view(np.uint8)
    return words, np.ascontiguousarray(byte.astype(np.uint8).reshape(k // 512, 16, n))


def unpack_weight(words, scales):
    g, p, n, _ = words.shape
    vals = np.ascontiguousarray(words).view(ml_dtypes.float8_e4m3fn).astype(np.float64) * np.repeat(np.exp2(scales.astype(np.float64) - 127.0), 8, axis=1)[..., None]
    return vals.transpose(0, 1, 3, 2).reshape(g * 512, n)


K, T, S, H, J, C = 512, 2048, 512, 512, 512, 512


def setup_inputs():
    n = np.random.standard_normal
    s = mx_kscale(K)[:, None]
    packed_xT = pack_weight(n((K, T)) * s)
    return {
        "x_words": packed_xT[0],
        "x_scales": packed_xT[1],
        "w1": (n((K, H)) / np.sqrt(K) / s).astype(np.float32),
        "tab": n((H, J)).astype(np.float32),
        "gs": (np.random.uniform(0.5, 1.5, (K, 1)) / s).astype(np.float32),
        "wb": (n((K, S)) / np.sqrt(K) / s).astype(np.float32),
        "tau": np.random.uniform(0.3, 0.9, (C, 1)).astype(np.float32),
        "offs": striped(np.random.permutation(T)[:S]),
        "n1": striped(np.random.randint(0, J, S)),
        "n2": striped(np.random.permutation(S)),
        "cand": striped(np.random.permutation(T)[:C]),
        "cb": striped(np.random.permutation(T)[:C]),
        "n3": striped(np.random.permutation(S)),
        "n4": striped(np.random.permutation(S)),
    }


def reference(x_words, x_scales, w1, tab, gs, wb, tau, offs, n1, n2, cand, cb, n3, n4):
    x_cb = unpack_weight(x_words, x_scales)[:, unstriped(cb)]
    b = x_cb.T @ mxq(f64(wb), 0, "e4m3")
    top = b.max(axis=1, keepdims=True)
    ea = np.exp(f64(tau) * (b[:, unstriped(n3)] - top))
    x_cand = unpack_weight(x_words, x_scales)[:, unstriped(cand)]
    xq = unpack_weight(x_words, x_scales)[:, unstriped(offs)]
    y = mxq(f64(w1), 0, "e4m3").T @ xq
    z = f64(gs) * (np.maximum(y + f64(tab)[:, unstriped(n1)], y[:, unstriped(n2)]))
    a = 0.0625 * ((x_cand.T @ mxq(z, 0, "e4m3")))
    return (2.0 * ea) * (a - a[:, unstriped(n4)]) - (0.5 * b)

@@ -1,0 +1,231 @@
+from contextlib import ExitStack
+
+import concourse.mybir as mybir
+
+K, T, S, H, C = 512, 2048, 512, 512, 512
+FLOPS = 3 * 2 * K * S * H
+
+F32 = mybir.dt.float32
+BF16 = mybir.dt.bfloat16
+I32 = mybir.dt.int32
+U32 = mybir.dt.uint32
+U16 = mybir.dt.uint16
+U8 = mybir.dt.uint8
+FP8X4 = mybir.dt.float8_e4m3fn_x4
+ALU = mybir.AluOpType
+ACT = mybir.ActivationFunctionType
+
+P = 128
+PACK = 4
+TILES = 4
+HALF = S // 2
+HALF_COLS = HALF // 16
+
+
+def tile_picked_cdswpxbkind_none_p_kernel(
+    tc, x_words, x_scales, w1, tab, gs, wb, tau, offs, n1, n2, cand, cb, n3, n4, out
+):
+    nc = tc.nc
+    with ExitStack() as ctx:
+        keep = ctx.enter_context(tc.tile_pool(name="keep", bufs=1))
+        psum = ctx.enter_context(tc.psum_pool(name="psum", bufs=1))
+
+        def sb(name, shape, dtype):
+            return keep.tile(shape, dtype, name=name, align_bytes=64)
+
+        def cols(h):
+            return slice(h * HALF, (h + 1) * HALF)
+
+        def half_list(lst, h):
+            return lst[:, h * HALF_COLS : (h + 1) * HALF_COLS]
+
+        lists = {}
+
+        def load_list(name, src):
+            lists[name] = keep.tile([P, S // 16], U16, name="list_" + name)
+            nc.sync.dma_start(lists[name][:], src)
+
+        def block(i):
+            return slice(i * P, (i + 1) * P)
+
+        def planes(name, dtype=F32):
+            return [sb("%s%d" % (name, i), [P, S], dtype) for i in range(TILES)]
+
+        def mx(bank, lhs_codes, lhs_scales, rhs_codes, rhs_scales):
+            nc.tensor.matmul_mx(
+                out=bank,
+                lhsT=lhs_codes.bitcast(FP8X4),
+                lhsT_scale=lhs_scales,
+                rhs=rhs_codes.bitcast(FP8X4),
+                rhs_scale=rhs_scales,
+                start=True,
+                stop=True,
+            )
+
+        scale_table = sb("scale_table", [P, T], U8)
+        nc.vector.memset(scale_table[:].bitcast(I32), 0)
+        for q in range(4):
+            nc.scalar.dma_start(
+                out=scale_table[32 * q : 32 * q + 4, :].bitcast(I32),
+                in_=x_scales[0, 4 * q : 4 * q + 4, :].bitcast(I32),
+            )
+        for name, src in (("offs", offs), ("n1", n1), ("cb", cb), ("cand", cand)):
+            load_list(name, src)
+        tab_rows = tab.rearrange("(p t) j -> t p j", t=PACK)
+        tab_win = planes("tab_win")
+        w1_rows = w1.rearrange("(p j) c -> p j c", j=PACK)
+        w1_raw = [sb("w1_raw%d" % h, [P, PACK, HALF], F32) for h in range(2)]
+        word_table = sb("word_table", [P, T], U32)
+        wb_raw = sb("wb_raw", [P, PACK, S], F32)
+        gs_sb = sb("gs_sb", [P, PACK], F32)
+        tau_sb = sb("tau_sb", [P, TILES], F32)
+        nc.sync.dma_start(out=tab_win[0][:], in_=tab_rows[0])
+        nc.sync.dma_start(out=w1_raw[0][:], in_=w1_rows[:, :, cols(0)])
+        nc.sync.dma_start(out=tab_win[1][:], in_=tab_rows[1])
+        nc.sync.dma_start(out=tab_win[2][:], in_=tab_rows[2])
+        nc.sync.dma_start(
+            out=word_table[:].bitcast(I32),
+            in_=x_words[0].rearrange("p n t -> p (n t)").bitcast(I32),
+        )
+        nc.sync.dma_start(out=w1_raw[1][:], in_=w1_rows[:, :, cols(1)])
+        nc.sync.dma_start(out=tab_win[3][:], in_=tab_rows[3])
+        load_list("n2", n2)
+        nc.sync.dma_start(out=wb_raw[:], in_=wb.rearrange("(p j) c -> p j c", j=PACK))
+        nc.sync.dma_start(out=gs_sb[:], in_=gs.rearrange("(p t) o -> p (t o)", t=PACK))
+        load_list("n3", n3)
+        load_list("n4", n4)
+        with nc.allow_non_contiguous_dma(reason="one rate a partition for each block of rows"):
+            nc.sync.dma_start(out=tau_sb[:], in_=tau.rearrange("(i p) o -> p (i o)", p=P))
+
+        words = {name: sb("words_" + name, [P, S], U32) for name in ("offs", "cb", "cand")}
+        scales = {name: sb("scales_" + name, [P, S], U8) for name in ("offs", "cb", "cand")}
+
+        def pick_scales(name):
+            nc.vector.tensor_copy(scales[name][:], scale_table[:].indirect(lists[name][:]))
+
+        def pick_words(name):
+            nc.vector.tensor_copy(words[name][:], word_table[:].indirect(lists[name][:]))
+
+        tab_at, y_win, y_at, first, larger = [planes(n) for n in ("tab_at", "y_win", "y_at", "first", "larger")]
+        b_win, ea, a_win, a_at, diff, prod = [planes(n) for n in ("b_win", "ea", "a_win", "a_at", "diff", "prod")]
+        w1_bf = sb("w1_bf", [P, H * PACK], BF16)
+        w1_codes = sb("w1_codes", [P, H], U32)
+        w1_scales = sb("w1_scales", [P, H], U8)
+        wb_bf = sb("wb_bf", [P, S * PACK], BF16)
+        wb_codes = sb("wb_codes", [P, S], U32)
+        wb_scales = sb("wb_scales", [P, S], U8)
+        z_planes = [sb("z_planes%d" % h, [P, PACK, HALF], BF16) for h in range(2)]
+        z_bf = [sb("z_bf%d" % h, [P, HALF * PACK], BF16) for h in range(2)]
+        z_codes = sb("z_codes", [P, S], U32)
+        z_scales = sb("z_scales", [P, S], U8)
+        top = sb("top", [P, TILES], F32)
+        shift = sb("shift", [P, TILES], F32)
+        res = [[sb("res%d_%d" % (i, h), [P, HALF], F32) for h in range(2)] for i in range(TILES)]
+
+        def fetch(dst, win, name):
+            for h in range(2):
+                nc.scalar.activation(dst[:, cols(h)], win[:].indirect(half_list(lists[name], h)), ACT.Copy)
+
+        def round_w1(h):
+            dealt = w1_bf[:].rearrange("p (t m j) -> p m j t", t=PACK, j=PACK)
+            nc.scalar.copy(
+                out=dealt[:, h * (P // 2) : (h + 1) * (P // 2)],
+                in_=w1_raw[h][:].rearrange("p j (m t) -> p m j t", t=PACK),
+            )
+
+        for name in ("offs", "cb", "cand"):
+            pick_scales(name)
+        fetch(tab_at[0], tab_win[0], "n1")
+        round_w1(0)
+        fetch(tab_at[1], tab_win[1], "n1")
+        fetch(tab_at[2], tab_win[2], "n1")
+        round_w1(1)
+        pick_words("offs")
+        nc.vector.quantize_mx(out=w1_codes[:].bitcast(FP8X4), scales=w1_scales[:], in_=w1_bf[:])
+        fetch(tab_at[3], tab_win[3], "n1")
+        pick_words("cb")
+        pick_words("cand")
+
+        y_bank = []
+        for t in range(TILES):
+            bank = psum.tile([P, S], F32, name="y_bank%d" % t, tag="bank%d" % t)
+            mx(bank[:], w1_codes[:, block(t)], w1_scales[:, block(t)], words["offs"][:], scales["offs"][:])
+            y_bank.append(bank)
+
+        def z_plane(t):
+            nc.scalar.copy(out=y_win[t][:], in_=y_bank[t][:])
+            fetch(y_at[t], y_win[t], "n2")
+            nc.vector.tensor_tensor(first[t][:], y_bank[t][:], tab_at[t][:], ALU.add)
+            for h in range(2):
+                nc.vector.tensor_tensor(larger[t][:, cols(h)], first[t][:, cols(h)], y_at[t][:, cols(h)], ALU.max)
+            for h in range(2):
+                nc.vector.tensor_scalar(
+                    z_planes[h][:, t, :], larger[t][:, cols(h)], gs_sb[:, t : t + 1], None, ALU.mult
+                )
+
+        b_bank = [psum.tile([P, S], F32, name="b_bank%d" % i, tag="bank%d" % (TILES + i)) for i in range(TILES)]
+
+        def b_pair(pair):
+            both = slice(2 * pair, 2 * pair + 2)
+            for i in (2 * pair, 2 * pair + 1):
+                nc.vector.tensor_scalar(
+                    b_win[i][:], b_bank[i][:], 1.0, None, ALU.mult, ALU.max, accum_out=top[:, i : i + 1]
+                )
+            nc.vector.scalar_tensor_tensor(shift[:, both], top[:, both], -1.0, tau_sb[:, both], ALU.mult, ALU.mult)
+
+        def weights(i):
+            for h in range(2):
+                nc.scalar.activation(
+                    ea[i][:, cols(h)],
+                    b_win[i][:].indirect(half_list(lists["n3"], h)),
+                    ACT.Exp,
+                    bias=shift[:, i : i + 1],
+                    scale=tau_sb[:, i : i + 1],
+                )
+
+        z_plane(0)
+        nc.vector.tensor_copy(
+            out=wb_bf[:].rearrange("p (c i j) -> p c j i", i=4, j=PACK),
+            in_=wb_raw[:].rearrange("p j (c i) -> p c j i", i=4),
+        )
+        z_plane(1)
+        nc.vector.quantize_mx(out=wb_codes[:].bitcast(FP8X4), scales=wb_scales[:], in_=wb_bf[:])
+        for i in range(TILES):
+            mx(b_bank[i][:], words["cb"][:, block(i)], scales["cb"][:, block(i)], wb_codes[:], wb_scales[:])
+        z_plane(2)
+        b_pair(0)
+        z_plane(3)
+        for h in range(2):
+            nc.vector.tensor_copy(
+                out=z_bf[h][:].rearrange("p (c i t) -> p c t i", i=4, t=PACK),
+                in_=z_planes[h][:].rearrange("p t (c i) -> p c t i", i=4),
+            )
+        for h in range(2):
+            nc.vector.quantize_mx(out=z_codes[:, cols(h)].bitcast(FP8X4), scales=z_scales[:, cols(h)], in_=z_bf[h][:])
+        b_pair(1)
+
+        a_bank = []
+        for i in range(TILES):
+            bank = psum.tile([P, S], F32, name="a_bank%d" % i, tag="bank%d" % i)
+            for h in range(2):
+                mx(bank[:, cols(h)], words["cand"][:, block(i)], scales["cand"][:, block(i)],
+                   z_codes[:, cols(h)], z_scales[:, cols(h)])
+            a_bank.append(bank)
+        weights(0)
+        weights(1)
+        for i in range(TILES):
+            nc.scalar.copy(out=a_win[i][:], in_=a_bank[i][:])
+            fetch(a_at[i], a_win[i], "n4")
+            if i < 2:
+                weights(i + 2)
+            for h in range(2):
+                nc.vector.tensor_tensor(diff[i][:, cols(h)], a_bank[i][:, cols(h)], a_at[i][:, cols(h)], ALU.subtract)
+            for h in range(2):
+                nc.vector.scalar_tensor_tensor(
+                    prod[i][:, cols(h)], diff[i][:, cols(h)], 0.125, ea[i][:, cols(h)], ALU.mult, ALU.mult
+                )
+            for h in range(2):
+                nc.vector.scalar_tensor_tensor(
+                    res[i][h][:], b_bank[i][:, cols(h)], -0.5, prod[i][:, cols(h)], ALU.mult, ALU.add
+                )
+                nc.sync.dma_start(out=out[block(i), cols(h)], in_=res[i][h][:])

@@ -2,7 +2,7 @@ from contextlib import ExitStack
 
 import concourse.mybir as mybir
 
-K, T, S, H, C = 512, 2048, 512, 512, 512
+K, T, S, H = 512, 2048, 512, 512
 FLOPS = 3 * 2 * K * S * H
 
 F32 = mybir.dt.float32
@@ -17,9 +17,14 @@ ACT = mybir.ActivationFunctionType
 
 P = 128
 PACK = 4
-TILES = 4
+BLOCKS = 4
+LAST = BLOCKS - 1
 HALF = S // 2
-HALF_COLS = HALF // 16
+LIST_COLS = S // 16
+SPARE = 32
+RUN = 4
+A_SCALE = 2.0 * 0.0625
+PLANES_WEIGHED_ON_SCALAR = 2
 
 
 def tile_picked_cdswpxbkind_none_p_kernel(
@@ -30,202 +35,223 @@ def tile_picked_cdswpxbkind_none_p_kernel(
         keep = ctx.enter_context(tc.tile_pool(name="keep", bufs=1))
         psum = ctx.enter_context(tc.psum_pool(name="psum", bufs=1))
 
-        def sb(name, shape, dtype):
-            return keep.tile(shape, dtype, name=name, align_bytes=64)
+        def sbuf(name, shape, dtype, after=None):
+            return keep.tile(shape, dtype, name=name, tag=after or name, align_bytes=64)
 
-        def cols(h):
+        def four(name, width):
+            return [sbuf("%s%d" % (name, i), [P, width], F32) for i in range(BLOCKS)]
+
+        def half(h):
             return slice(h * HALF, (h + 1) * HALF)
-
-        def half_list(lst, h):
-            return lst[:, h * HALF_COLS : (h + 1) * HALF_COLS]
-
-        lists = {}
-
-        def load_list(name, src):
-            lists[name] = keep.tile([P, S // 16], U16, name="list_" + name)
-            nc.sync.dma_start(lists[name][:], src)
 
         def block(i):
             return slice(i * P, (i + 1) * P)
 
-        def planes(name, dtype=F32):
-            return [sb("%s%d" % (name, i), [P, S], dtype) for i in range(TILES)]
-
-        def mx(bank, lhs_codes, lhs_scales, rhs_codes, rhs_scales):
+        def product(bank, lhs_words, lhs_scales, rhs_words, rhs_scales):
             nc.tensor.matmul_mx(
                 out=bank,
-                lhsT=lhs_codes.bitcast(FP8X4),
+                lhsT=lhs_words.bitcast(FP8X4),
                 lhsT_scale=lhs_scales,
-                rhs=rhs_codes.bitcast(FP8X4),
+                rhs=rhs_words.bitcast(FP8X4),
                 rhs_scale=rhs_scales,
                 start=True,
                 stop=True,
             )
 
-        scale_table = sb("scale_table", [P, T], U8)
+        scale_table = sbuf("scale_table", [P, T], U8)
+        word_table = sbuf("word_table", [P, T], U32)
+        tab_win = four("tab_win", S + SPARE)
+        w1_raw = [sbuf("w1_raw%d" % h, [P, PACK, HALF], F32) for h in range(2)]
+        wb_raw = sbuf("wb_raw", [P, PACK, S], F32)
+        gs_sb = sbuf("gs_sb", [P, PACK], F32)
+        tau_sb = sbuf("tau_sb", [P, BLOCKS], F32)
+        lists = {}
+        tab_planes = tab.rearrange("(p t) j -> t p j", t=PACK)
+        w1_rows = w1.rearrange("(p j) c -> p j c", j=PACK)
+
+        def load_list(name, source):
+            lists[name] = keep.tile([P, LIST_COLS], U16, name="list_" + name)
+            nc.sync.dma_start(lists[name][:], source)
+
+        def load_tab(t):
+            nc.sync.dma_start(out=tab_win[t][:, :S], in_=tab_planes[t])
+
+        def load_w1(h):
+            nc.sync.dma_start(out=w1_raw[h][:], in_=w1_rows[:, :, half(h)])
+
         nc.vector.memset(scale_table[:].bitcast(I32), 0)
+        for t in range(PACK):
+            nc.vector.memset(tab_win[t][:, S:], 0.0)
+
+        load_w1(0)
+        load_list("offs", offs)
+        load_list("cb", cb)
         for q in range(4):
-            nc.scalar.dma_start(
+            nc.sync.dma_start(
                 out=scale_table[32 * q : 32 * q + 4, :].bitcast(I32),
                 in_=x_scales[0, 4 * q : 4 * q + 4, :].bitcast(I32),
             )
-        for name, src in (("offs", offs), ("n1", n1), ("cb", cb), ("cand", cand)):
-            load_list(name, src)
-        tab_rows = tab.rearrange("(p t) j -> t p j", t=PACK)
-        tab_win = planes("tab_win")
-        w1_rows = w1.rearrange("(p j) c -> p j c", j=PACK)
-        w1_raw = [sb("w1_raw%d" % h, [P, PACK, HALF], F32) for h in range(2)]
-        word_table = sb("word_table", [P, T], U32)
-        wb_raw = sb("wb_raw", [P, PACK, S], F32)
-        gs_sb = sb("gs_sb", [P, PACK], F32)
-        tau_sb = sb("tau_sb", [P, TILES], F32)
-        nc.sync.dma_start(out=tab_win[0][:], in_=tab_rows[0])
-        nc.sync.dma_start(out=w1_raw[0][:], in_=w1_rows[:, :, cols(0)])
-        nc.sync.dma_start(out=tab_win[1][:], in_=tab_rows[1])
-        nc.sync.dma_start(out=tab_win[2][:], in_=tab_rows[2])
         nc.sync.dma_start(
             out=word_table[:].bitcast(I32),
             in_=x_words[0].rearrange("p n t -> p (n t)").bitcast(I32),
         )
-        nc.sync.dma_start(out=w1_raw[1][:], in_=w1_rows[:, :, cols(1)])
-        nc.sync.dma_start(out=tab_win[3][:], in_=tab_rows[3])
+        load_list("n1", n1)
+        load_tab(0)
+        load_list("cand", cand)
+        load_w1(1)
+        for t in range(1, PACK):
+            load_tab(t)
         load_list("n2", n2)
         nc.sync.dma_start(out=wb_raw[:], in_=wb.rearrange("(p j) c -> p j c", j=PACK))
         nc.sync.dma_start(out=gs_sb[:], in_=gs.rearrange("(p t) o -> p (t o)", t=PACK))
-        load_list("n3", n3)
-        load_list("n4", n4)
         with nc.allow_non_contiguous_dma(reason="one rate a partition for each block of rows"):
             nc.sync.dma_start(out=tau_sb[:], in_=tau.rearrange("(i p) o -> p (i o)", p=P))
+        load_list("n3", n3)
+        load_list("n4", n4)
 
-        words = {name: sb("words_" + name, [P, S], U32) for name in ("offs", "cb", "cand")}
-        scales = {name: sb("scales_" + name, [P, S], U8) for name in ("offs", "cb", "cand")}
+        ya_win = four("ya_win", 2 * S)
+        b_win = four("b_win", 2 * S)
+        tab_at = [win[:, S:] for win in ya_win]
+        y_at = [win[:, S:] for win in b_win]
+        larger = four("larger", S)
+        a_at = four("a_at", S)
+        weighed = four("weighed", S)
+        w1_bf = sbuf("w1_bf", [P, H * PACK], BF16)
+        w1_words = sbuf("w1_words", [P, H], U32)
+        w1_scales = sbuf("w1_scales", [P, H], U8)
+        wb_words = sbuf("wb_words", [P, S], U32)
+        wb_scales = sbuf("wb_scales", [P, S], U8)
+        z_planes = sbuf("z_planes", [P, PACK, S], BF16)
+        z_bf = [sbuf("z_bf%d" % h, [P, HALF * PACK], BF16) for h in range(2)]
+        z_words = sbuf("z_words", [P, S], U32)
+        z_scales = sbuf("z_scales", [P, S], U8)
+        shift = sbuf("shift", [P, BLOCKS], F32)
+        result = [[sbuf("result%d_%d" % (i, h), [P, HALF], F32) for h in range(2)] for i in range(BLOCKS)]
+        y_bank = [psum.tile([P, S], F32, name="y_bank%d" % t, tag="bank%d" % t) for t in range(PACK)]
+        b_bank = [psum.tile([P, S], F32, name="b_bank%d" % i, tag="bank%d" % (PACK + i)) for i in range(BLOCKS)]
+        picked_words, picked_scales, ea = {}, {}, {}
 
         def pick_scales(name):
-            nc.vector.tensor_copy(scales[name][:], scale_table[:].indirect(lists[name][:]))
+            picked_scales[name] = sbuf("scales_" + name, [P, S], U8)
+            nc.vector.tensor_copy(picked_scales[name][:], scale_table[:].indirect(lists[name][:]))
 
-        def pick_words(name):
-            nc.vector.tensor_copy(words[name][:], word_table[:].indirect(lists[name][:]))
+        def pick_words(name, after=None):
+            picked_words[name] = sbuf("words_" + name, [P, S], U32, after)
+            nc.vector.tensor_copy(picked_words[name][:], word_table[:].indirect(lists[name][:]))
 
-        tab_at, y_win, y_at, first, larger = [planes(n) for n in ("tab_at", "y_win", "y_at", "first", "larger")]
-        b_win, ea, a_win, a_at, diff, prod = [planes(n) for n in ("b_win", "ea", "a_win", "a_at", "diff", "prod")]
-        w1_bf = sb("w1_bf", [P, H * PACK], BF16)
-        w1_codes = sb("w1_codes", [P, H], U32)
-        w1_scales = sb("w1_scales", [P, H], U8)
-        wb_bf = sb("wb_bf", [P, S * PACK], BF16)
-        wb_codes = sb("wb_codes", [P, S], U32)
-        wb_scales = sb("wb_scales", [P, S], U8)
-        z_planes = [sb("z_planes%d" % h, [P, PACK, HALF], BF16) for h in range(2)]
-        z_bf = [sb("z_bf%d" % h, [P, HALF * PACK], BF16) for h in range(2)]
-        z_codes = sb("z_codes", [P, S], U32)
-        z_scales = sb("z_scales", [P, S], U8)
-        top = sb("top", [P, TILES], F32)
-        shift = sb("shift", [P, TILES], F32)
-        res = [[sb("res%d_%d" % (i, h), [P, HALF], F32) for h in range(2)] for i in range(TILES)]
+        def fetch(dst, win, offsets):
+            nc.scalar.activation(dst, win[:].indirect(offsets), ACT.Copy)
 
-        def fetch(dst, win, name):
-            for h in range(2):
-                nc.scalar.activation(dst[:, cols(h)], win[:].indirect(half_list(lists[name], h)), ACT.Copy)
+        pick_scales("offs")
+        pick_words("offs")
+        fetch(tab_at[0], tab_win[0], lists["n1"][:])
+        w1_dealt = w1_bf[:].rearrange("p (t m j) -> p m j t", t=PACK, j=PACK)
+        for h in range(2):
+            nc.scalar.activation(
+                w1_dealt[:, h * (P // 2) : (h + 1) * (P // 2)],
+                w1_raw[h][:].rearrange("p j (m t) -> p m j t", t=PACK),
+                ACT.Copy,
+            )
+        nc.vector.quantize_mx(out=w1_words[:].bitcast(FP8X4), scales=w1_scales[:], in_=w1_bf[:])
+        for t in range(PACK):
+            product(
+                y_bank[t][:], w1_words[:, block(t)], w1_scales[:, block(t)],
+                picked_words["offs"][:], picked_scales["offs"][:],
+            )
+        pick_scales("cb")
+        pick_words("cb")
+        for t in range(1, PACK):
+            fetch(tab_at[t], tab_win[t], lists["n1"][:])
+        pick_scales("cand")
+        pick_words("cand", after="w1_raw1")
 
-        def round_w1(h):
-            dealt = w1_bf[:].rearrange("p (t m j) -> p m j t", t=PACK, j=PACK)
-            nc.scalar.copy(
-                out=dealt[:, h * (P // 2) : (h + 1) * (P // 2)],
-                in_=w1_raw[h][:].rearrange("p j (m t) -> p m j t", t=PACK),
+        wb_bf = sbuf("wb_bf", [P, S * PACK], BF16, after="w1_bf")
+        nc.vector.tensor_copy(
+            out=wb_bf[:].rearrange("p (c i j) -> p c j i", i=RUN, j=PACK),
+            in_=wb_raw[:].rearrange("p j (c i) -> p c j i", i=RUN),
+        )
+        nc.vector.quantize_mx(out=wb_words[:].bitcast(FP8X4), scales=wb_scales[:], in_=wb_bf[:])
+        for i in range(BLOCKS):
+            product(
+                b_bank[i][:], picked_words["cb"][:, block(i)], picked_scales["cb"][:, block(i)],
+                wb_words[:], wb_scales[:],
             )
 
-        for name in ("offs", "cb", "cand"):
-            pick_scales(name)
-        fetch(tab_at[0], tab_win[0], "n1")
-        round_w1(0)
-        fetch(tab_at[1], tab_win[1], "n1")
-        fetch(tab_at[2], tab_win[2], "n1")
-        round_w1(1)
-        pick_words("offs")
-        nc.vector.quantize_mx(out=w1_codes[:].bitcast(FP8X4), scales=w1_scales[:], in_=w1_bf[:])
-        fetch(tab_at[3], tab_win[3], "n1")
-        pick_words("cb")
-        pick_words("cand")
+        def b_out_of_psum(i, after=None):
+            top = sbuf("top%d" % i, [P, 1], F32, after)
+            nc.vector.tensor_scalar(b_win[i][:, :S], b_bank[i][:], 1.0, None, ALU.mult, ALU.max, accum_out=top[:])
+            nc.vector.tensor_scalar(shift[:, i : i + 1], top[:], tau_sb[:, i : i + 1], -1.0, ALU.mult, ALU.mult)
 
-        y_bank = []
-        for t in range(TILES):
-            bank = psum.tile([P, S], F32, name="y_bank%d" % t, tag="bank%d" % t)
-            mx(bank[:], w1_codes[:, block(t)], w1_scales[:, block(t)], words["offs"][:], scales["offs"][:])
-            y_bank.append(bank)
+        def exponentials(i, after=None):
+            ea[i] = sbuf("ea%d" % i, [P, S], F32, after)
+            nc.scalar.activation(
+                ea[i][:],
+                b_win[i][:].indirect(lists["n3"][:]),
+                ACT.Exp,
+                bias=shift[:, i : i + 1],
+                scale=tau_sb[:, i : i + 1],
+            )
 
-        def z_plane(t):
-            nc.scalar.copy(out=y_win[t][:], in_=y_bank[t][:])
-            fetch(y_at[t], y_win[t], "n2")
-            nc.vector.tensor_tensor(first[t][:], y_bank[t][:], tab_at[t][:], ALU.add)
-            for h in range(2):
-                nc.vector.tensor_tensor(larger[t][:, cols(h)], first[t][:, cols(h)], y_at[t][:, cols(h)], ALU.max)
-            for h in range(2):
-                nc.vector.tensor_scalar(
-                    z_planes[h][:, t, :], larger[t][:, cols(h)], gs_sb[:, t : t + 1], None, ALU.mult
-                )
+        for t in range(PACK):
+            nc.scalar.copy(out=ya_win[t][:, :S], in_=y_bank[t][:])
+            fetch(y_at[t], ya_win[t], lists["n2"][:])
+        for t in range(PACK):
+            summed = sbuf("summed%d" % t, [P, S], F32, after=("wb_raw", "w1_bf")[t % 2])
+            nc.vector.tensor_tensor(summed[:], y_bank[t][:], tab_at[t], ALU.add)
+            pieces = [half(0), half(1)] if t == LAST else [slice(0, S)]
+            for cols in pieces:
+                nc.vector.tensor_tensor(larger[t][:, cols], summed[:, cols], y_at[t][:, cols], ALU.max)
+            for cols in pieces:
+                if t < PLANES_WEIGHED_ON_SCALAR:
+                    nc.scalar.mul(z_planes[:, t, cols], larger[t][:, cols], gs_sb[:, t : t + 1])
+                else:
+                    nc.vector.tensor_scalar(
+                        z_planes[:, t, cols], larger[t][:, cols], gs_sb[:, t : t + 1], None, ALU.mult
+                    )
+            if t < LAST:
+                b_out_of_psum(t)
 
-        b_bank = [psum.tile([P, S], F32, name="b_bank%d" % i, tag="bank%d" % (TILES + i)) for i in range(TILES)]
-
-        def b_pair(pair):
-            both = slice(2 * pair, 2 * pair + 2)
-            for i in (2 * pair, 2 * pair + 1):
-                nc.vector.tensor_scalar(
-                    b_win[i][:], b_bank[i][:], 1.0, None, ALU.mult, ALU.max, accum_out=top[:, i : i + 1]
-                )
-            nc.vector.scalar_tensor_tensor(shift[:, both], top[:, both], -1.0, tau_sb[:, both], ALU.mult, ALU.mult)
-
-        def weights(i):
-            for h in range(2):
-                nc.scalar.activation(
-                    ea[i][:, cols(h)],
-                    b_win[i][:].indirect(half_list(lists["n3"], h)),
-                    ACT.Exp,
-                    bias=shift[:, i : i + 1],
-                    scale=tau_sb[:, i : i + 1],
-                )
-
-        z_plane(0)
-        nc.vector.tensor_copy(
-            out=wb_bf[:].rearrange("p (c i j) -> p c j i", i=4, j=PACK),
-            in_=wb_raw[:].rearrange("p j (c i) -> p c j i", i=4),
-        )
-        z_plane(1)
-        nc.vector.quantize_mx(out=wb_codes[:].bitcast(FP8X4), scales=wb_scales[:], in_=wb_bf[:])
-        for i in range(TILES):
-            mx(b_bank[i][:], words["cb"][:, block(i)], scales["cb"][:, block(i)], wb_codes[:], wb_scales[:])
-        z_plane(2)
-        b_pair(0)
-        z_plane(3)
         for h in range(2):
             nc.vector.tensor_copy(
-                out=z_bf[h][:].rearrange("p (c i t) -> p c t i", i=4, t=PACK),
-                in_=z_planes[h][:].rearrange("p t (c i) -> p c t i", i=4),
+                out=z_bf[h][:].rearrange("p (c i t) -> p c t i", i=RUN, t=PACK),
+                in_=z_planes[:, :, half(h)].rearrange("p t (c i) -> p c t i", i=RUN),
             )
         for h in range(2):
-            nc.vector.quantize_mx(out=z_codes[:, cols(h)].bitcast(FP8X4), scales=z_scales[:, cols(h)], in_=z_bf[h][:])
-        b_pair(1)
-
+            nc.vector.quantize_mx(out=z_words[:, half(h)].bitcast(FP8X4), scales=z_scales[:, half(h)], in_=z_bf[h][:])
         a_bank = []
-        for i in range(TILES):
-            bank = psum.tile([P, S], F32, name="a_bank%d" % i, tag="bank%d" % i)
-            for h in range(2):
-                mx(bank[:, cols(h)], words["cand"][:, block(i)], scales["cand"][:, block(i)],
-                   z_codes[:, cols(h)], z_scales[:, cols(h)])
-            a_bank.append(bank)
-        weights(0)
-        weights(1)
-        for i in range(TILES):
-            nc.scalar.copy(out=a_win[i][:], in_=a_bank[i][:])
-            fetch(a_at[i], a_win[i], "n4")
-            if i < 2:
-                weights(i + 2)
-            for h in range(2):
-                nc.vector.tensor_tensor(diff[i][:, cols(h)], a_bank[i][:, cols(h)], a_at[i][:, cols(h)], ALU.subtract)
+        for i in range(BLOCKS):
+            a_bank.append(psum.tile([P, S], F32, name="a_bank%d" % i, tag="bank%d" % i))
+            product(
+                a_bank[i][:], picked_words["cand"][:, block(i)], picked_scales["cand"][:, block(i)],
+                z_words[:], z_scales[:],
+            )
+        b_out_of_psum(LAST, after="z_bf0")
+
+        exponentials(0, after="larger1")
+        exponentials(1, after="w1_bf")
+        exponentials(2)
+
+        nc.scalar.mul(ya_win[0][:, :S], a_bank[0][:], A_SCALE)
+        for i in range(1, BLOCKS):
+            nc.vector.tensor_scalar(ya_win[i][:, :S], a_bank[i][:], A_SCALE, None, ALU.mult)
+        for i in range(BLOCKS):
+            if i == LAST:
+                exponentials(LAST, after="ya_win1")
+            if i in (0, LAST):
+                for h in range(2):
+                    offsets = lists["n4"][:, h * (LIST_COLS // 2) : (h + 1) * (LIST_COLS // 2)]
+                    fetch(a_at[i][:, half(h)], ya_win[i], offsets)
+            else:
+                fetch(a_at[i][:], ya_win[i], lists["n4"][:])
+            diff = sbuf("diff%d" % i, [P, S], F32, after="diff0")
             for h in range(2):
                 nc.vector.scalar_tensor_tensor(
-                    prod[i][:, cols(h)], diff[i][:, cols(h)], 0.125, ea[i][:, cols(h)], ALU.mult, ALU.mult
+                    diff[:, half(h)], a_bank[i][:, half(h)], A_SCALE, a_at[i][:, half(h)], ALU.mult, ALU.subtract
                 )
             for h in range(2):
+                nc.vector.tensor_tensor(weighed[i][:, half(h)], diff[:, half(h)], ea[i][:, half(h)], ALU.mult)
+            for h in range(2):
                 nc.vector.scalar_tensor_tensor(
-                    res[i][h][:], b_bank[i][:, cols(h)], -0.5, prod[i][:, cols(h)], ALU.mult, ALU.add
+                    result[i][h][:], b_bank[i][:, half(h)], -0.5, weighed[i][:, half(h)], ALU.mult, ALU.add
                 )
-                nc.sync.dma_start(out=out[block(i), cols(h)], in_=res[i][h][:])
+                nc.sync.dma_start(out=out[block(i), half(h)], in_=result[i][h][:])

from contextlib import ExitStack

import concourse.mybir as mybir

K, T, S, H = 512, 2048, 512, 512
FLOPS = 3 * 2 * K * S * H

F32 = mybir.dt.float32
BF16 = mybir.dt.bfloat16
I32 = mybir.dt.int32
U32 = mybir.dt.uint32
U16 = mybir.dt.uint16
U8 = mybir.dt.uint8
FP8X4 = mybir.dt.float8_e4m3fn_x4
ALU = mybir.AluOpType
ACT = mybir.ActivationFunctionType

P = 128
PACK = 4
BLOCKS = 4
LAST = BLOCKS - 1
HALF = S // 2
LIST_COLS = S // 16
SPARE = 32
RUN = 4
A_SCALE = 2.0 * 0.0625
PLANES_WEIGHED_ON_SCALAR = 2


def tile_picked_cdswpxbkind_none_p_kernel(
    tc, x_words, x_scales, w1, tab, gs, wb, tau, offs, n1, n2, cand, cb, n3, n4, out
):
    nc = tc.nc
    with ExitStack() as ctx:
        keep = ctx.enter_context(tc.tile_pool(name="keep", bufs=1))
        psum = ctx.enter_context(tc.psum_pool(name="psum", bufs=1))

        def sbuf(name, shape, dtype, after=None):
            return keep.tile(shape, dtype, name=name, tag=after or name, align_bytes=64)

        def four(name, width):
            return [sbuf("%s%d" % (name, i), [P, width], F32) for i in range(BLOCKS)]

        def half(h):
            return slice(h * HALF, (h + 1) * HALF)

        def block(i):
            return slice(i * P, (i + 1) * P)

        def product(bank, lhs_words, lhs_scales, rhs_words, rhs_scales):
            nc.tensor.matmul_mx(
                out=bank,
                lhsT=lhs_words.bitcast(FP8X4),
                lhsT_scale=lhs_scales,
                rhs=rhs_words.bitcast(FP8X4),
                rhs_scale=rhs_scales,
                start=True,
                stop=True,
            )

        scale_table = sbuf("scale_table", [P, T], U8)
        word_table = sbuf("word_table", [P, T], U32)
        tab_win = four("tab_win", S + SPARE)
        w1_raw = [sbuf("w1_raw%d" % h, [P, PACK, HALF], F32) for h in range(2)]
        wb_raw = sbuf("wb_raw", [P, PACK, S], F32)
        gs_sb = sbuf("gs_sb", [P, PACK], F32)
        tau_sb = sbuf("tau_sb", [P, BLOCKS], F32)
        lists = {}
        tab_planes = tab.rearrange("(p t) j -> t p j", t=PACK)
        w1_rows = w1.rearrange("(p j) c -> p j c", j=PACK)

        def load_list(name, source):
            lists[name] = keep.tile([P, LIST_COLS], U16, name="list_" + name)
            nc.sync.dma_start(lists[name][:], source)

        def load_tab(t):
            nc.sync.dma_start(out=tab_win[t][:, :S], in_=tab_planes[t])

        def load_w1(h):
            nc.sync.dma_start(out=w1_raw[h][:], in_=w1_rows[:, :, half(h)])

        nc.vector.memset(scale_table[:].bitcast(I32), 0)
        for t in range(PACK):
            nc.vector.memset(tab_win[t][:, S:], 0.0)

        load_w1(0)
        load_list("offs", offs)
        load_list("cb", cb)
        for q in range(4):
            nc.sync.dma_start(
                out=scale_table[32 * q : 32 * q + 4, :].bitcast(I32),
                in_=x_scales[0, 4 * q : 4 * q + 4, :].bitcast(I32),
            )
        nc.sync.dma_start(
            out=word_table[:].bitcast(I32),
            in_=x_words[0].rearrange("p n t -> p (n t)").bitcast(I32),
        )
        load_list("n1", n1)
        load_tab(0)
        load_list("cand", cand)
        load_w1(1)
        for t in range(1, PACK):
            load_tab(t)
        load_list("n2", n2)
        nc.sync.dma_start(out=wb_raw[:], in_=wb.rearrange("(p j) c -> p j c", j=PACK))
        nc.sync.dma_start(out=gs_sb[:], in_=gs.rearrange("(p t) o -> p (t o)", t=PACK))
        with nc.allow_non_contiguous_dma(reason="one rate a partition for each block of rows"):
            nc.sync.dma_start(out=tau_sb[:], in_=tau.rearrange("(i p) o -> p (i o)", p=P))
        load_list("n3", n3)
        load_list("n4", n4)

        ya_win = four("ya_win", 2 * S)
        b_win = four("b_win", 2 * S)
        tab_at = [win[:, S:] for win in ya_win]
        y_at = [win[:, S:] for win in b_win]
        larger = four("larger", S)
        a_at = four("a_at", S)
        weighed = four("weighed", S)
        w1_bf = sbuf("w1_bf", [P, H * PACK], BF16)
        w1_words = sbuf("w1_words", [P, H], U32)
        w1_scales = sbuf("w1_scales", [P, H], U8)
        wb_words = sbuf("wb_words", [P, S], U32)
        wb_scales = sbuf("wb_scales", [P, S], U8)
        z_planes = sbuf("z_planes", [P, PACK, S], BF16)
        z_bf = [sbuf("z_bf%d" % h, [P, HALF * PACK], BF16) for h in range(2)]
        z_words = sbuf("z_words", [P, S], U32)
        z_scales = sbuf("z_scales", [P, S], U8)
        shift = sbuf("shift", [P, BLOCKS], F32)
        result = [[sbuf("result%d_%d" % (i, h), [P, HALF], F32) for h in range(2)] for i in range(BLOCKS)]
        y_bank = [psum.tile([P, S], F32, name="y_bank%d" % t, tag="bank%d" % t) for t in range(PACK)]
        b_bank = [psum.tile([P, S], F32, name="b_bank%d" % i, tag="bank%d" % (PACK + i)) for i in range(BLOCKS)]
        picked_words, picked_scales, ea = {}, {}, {}

        def pick_scales(name):
            picked_scales[name] = sbuf("scales_" + name, [P, S], U8)
            nc.vector.tensor_copy(picked_scales[name][:], scale_table[:].indirect(lists[name][:]))

        def pick_words(name, after=None):
            picked_words[name] = sbuf("words_" + name, [P, S], U32, after)
            nc.vector.tensor_copy(picked_words[name][:], word_table[:].indirect(lists[name][:]))

        def fetch(dst, win, offsets):
            nc.scalar.activation(dst, win[:].indirect(offsets), ACT.Copy)

        pick_scales("offs")
        pick_words("offs")
        fetch(tab_at[0], tab_win[0], lists["n1"][:])
        w1_dealt = w1_bf[:].rearrange("p (t m j) -> p m j t", t=PACK, j=PACK)
        for h in range(2):
            nc.scalar.activation(
                w1_dealt[:, h * (P // 2) : (h + 1) * (P // 2)],
                w1_raw[h][:].rearrange("p j (m t) -> p m j t", t=PACK),
                ACT.Copy,
            )
        nc.vector.quantize_mx(out=w1_words[:].bitcast(FP8X4), scales=w1_scales[:], in_=w1_bf[:])
        for t in range(PACK):
            product(
                y_bank[t][:], w1_words[:, block(t)], w1_scales[:, block(t)],
                picked_words["offs"][:], picked_scales["offs"][:],
            )
        pick_scales("cb")
        pick_words("cb")
        for t in range(1, PACK):
            fetch(tab_at[t], tab_win[t], lists["n1"][:])
        pick_scales("cand")
        pick_words("cand", after="w1_raw1")

        wb_bf = sbuf("wb_bf", [P, S * PACK], BF16, after="w1_bf")
        nc.vector.tensor_copy(
            out=wb_bf[:].rearrange("p (c i j) -> p c j i", i=RUN, j=PACK),
            in_=wb_raw[:].rearrange("p j (c i) -> p c j i", i=RUN),
        )
        nc.vector.quantize_mx(out=wb_words[:].bitcast(FP8X4), scales=wb_scales[:], in_=wb_bf[:])
        for i in range(BLOCKS):
            product(
                b_bank[i][:], picked_words["cb"][:, block(i)], picked_scales["cb"][:, block(i)],
                wb_words[:], wb_scales[:],
            )

        def b_out_of_psum(i, after=None):
            top = sbuf("top%d" % i, [P, 1], F32, after)
            nc.vector.tensor_scalar(b_win[i][:, :S], b_bank[i][:], 1.0, None, ALU.mult, ALU.max, accum_out=top[:])
            nc.vector.tensor_scalar(shift[:, i : i + 1], top[:], tau_sb[:, i : i + 1], -1.0, ALU.mult, ALU.mult)

        def exponentials(i, after=None):
            ea[i] = sbuf("ea%d" % i, [P, S], F32, after)
            nc.scalar.activation(
                ea[i][:],
                b_win[i][:].indirect(lists["n3"][:]),
                ACT.Exp,
                bias=shift[:, i : i + 1],
                scale=tau_sb[:, i : i + 1],
            )

        for t in range(PACK):
            nc.scalar.copy(out=ya_win[t][:, :S], in_=y_bank[t][:])
            fetch(y_at[t], ya_win[t], lists["n2"][:])
        for t in range(PACK):
            summed = sbuf("summed%d" % t, [P, S], F32, after=("wb_raw", "w1_bf")[t % 2])
            nc.vector.tensor_tensor(summed[:], y_bank[t][:], tab_at[t], ALU.add)
            pieces = [half(0), half(1)] if t == LAST else [slice(0, S)]
            for cols in pieces:
                nc.vector.tensor_tensor(larger[t][:, cols], summed[:, cols], y_at[t][:, cols], ALU.max)
            for cols in pieces:
                if t < PLANES_WEIGHED_ON_SCALAR:
                    nc.scalar.mul(z_planes[:, t, cols], larger[t][:, cols], gs_sb[:, t : t + 1])
                else:
                    nc.vector.tensor_scalar(
                        z_planes[:, t, cols], larger[t][:, cols], gs_sb[:, t : t + 1], None, ALU.mult
                    )
            if t < LAST:
                b_out_of_psum(t)

        for h in range(2):
            nc.vector.tensor_copy(
                out=z_bf[h][:].rearrange("p (c i t) -> p c t i", i=RUN, t=PACK),
                in_=z_planes[:, :, half(h)].rearrange("p t (c i) -> p c t i", i=RUN),
            )
        for h in range(2):
            nc.vector.quantize_mx(out=z_words[:, half(h)].bitcast(FP8X4), scales=z_scales[:, half(h)], in_=z_bf[h][:])
        a_bank = []
        for i in range(BLOCKS):
            a_bank.append(psum.tile([P, S], F32, name="a_bank%d" % i, tag="bank%d" % i))
            product(
                a_bank[i][:], picked_words["cand"][:, block(i)], picked_scales["cand"][:, block(i)],
                z_words[:], z_scales[:],
            )
        b_out_of_psum(LAST, after="z_bf0")

        exponentials(0, after="larger1")
        exponentials(1, after="w1_bf")
        exponentials(2)

        nc.scalar.mul(ya_win[0][:, :S], a_bank[0][:], A_SCALE)
        for i in range(1, BLOCKS):
            nc.vector.tensor_scalar(ya_win[i][:, :S], a_bank[i][:], A_SCALE, None, ALU.mult)
        for i in range(BLOCKS):
            if i == LAST:
                exponentials(LAST, after="ya_win1")
            if i in (0, LAST):
                for h in range(2):
                    offsets = lists["n4"][:, h * (LIST_COLS // 2) : (h + 1) * (LIST_COLS // 2)]
                    fetch(a_at[i][:, half(h)], ya_win[i], offsets)
            else:
                fetch(a_at[i][:], ya_win[i], lists["n4"][:])
            diff = sbuf("diff%d" % i, [P, S], F32, after="diff0")
            for h in range(2):
                nc.vector.scalar_tensor_tensor(
                    diff[:, half(h)], a_bank[i][:, half(h)], A_SCALE, a_at[i][:, half(h)], ALU.mult, ALU.subtract
                )
            for h in range(2):
                nc.vector.tensor_tensor(weighed[i][:, half(h)], diff[:, half(h)], ea[i][:, half(h)], ALU.mult)
            for h in range(2):
                nc.vector.scalar_tensor_tensor(
                    result[i][h][:], b_bank[i][:, half(h)], -0.5, weighed[i][:, half(h)], ALU.mult, ALU.add
                )
                nc.sync.dma_start(out=out[block(i), half(h)], in_=result[i][h][:])
